import numpy as np
import ml_dtypes


def mxq(x, axis, fmt="e4m3"):
    dtype, down = {"e4m3": (ml_dtypes.float8_e4m3fn, 7), "e5m2": (ml_dtypes.float8_e5m2, 14)}[fmt]
    v = np.moveaxis(np.asarray(x, np.float32).astype(ml_dtypes.bfloat16).astype(np.float64), axis, -1)
    blocks = v.reshape(v.shape[:-1] + (-1, 32))
    amax = np.abs(blocks).max(-1, keepdims=True)
    byte = np.maximum(np.where(amax > 0, np.frexp(amax)[1] - 1 + 127, 0) - down, 1)
    scale = np.exp2(byte - 127.0)
    codes = (blocks / scale).astype(np.float32).astype(dtype).astype(np.float64)
    return np.moveaxis((codes * scale).reshape(v.shape), -1, axis)


WIDE = False


def mx_kscale(k):
    if not WIDE:
        return np.ones(k)
    levels = np.array([10, -10, 5, -5, 0])
    if k % 512:
        return np.exp2(np.random.permutation(np.resize(levels, k // 32))).repeat(32)
    a = np.empty((k // 512, 16))
    for p in range(k // 512):
        a[p, :8] = np.random.permutation(np.resize(levels, 8))
        for g in range(8):
            far = levels[np.abs(levels - a[p, g]) >= 10]
            a[p, g + 8] = far[np.random.randint(len(far))]
    return np.exp2(a.ravel()).repeat(32)


def f64(x):
    return np.asarray(x).astype(np.float64)


def planes(y):
    n, m = y.shape
    v = y.astype(np.float32).astype(ml_dtypes.bfloat16).astype(np.float64).reshape(n // 32, 32, m)
    top = np.abs(v).max(1)
    byte = np.clip(np.where(top > 0, np.frexp(top)[1] - 1 + 127 - 7, 1), 1, 254)
    codes = (v * np.exp2(127.0 - byte)[:, None, :]).reshape(n, m).astype(np.float32).astype(ml_dtypes.float8_e4m3fn).view(np.uint8)
    words = codes.reshape(n // 512, 128, 4, m).transpose(0, 1, 3, 2)
    return np.ascontiguousarray(words), np.ascontiguousarray(byte.astype(np.uint8).reshape(n // 512, 16, m))


def split(x):
    m, e = np.frexp(f64(x))
    hi = np.ldexp(np.trunc(16.0 * m) / 16.0, e)
    return hi, f64(x) - hi


K, M, T = 2048, 512, 512


def setup_inputs():
    n = np.random.standard_normal
    s = mx_kscale(K)[:, None]
    return {
        "w": (n((K, M)) / np.sqrt(K) / s).astype(np.float32),
        "x": (n((K, T)) * s).astype(np.float32),
        "r": (n((512, 512))).astype(np.float32),
    }


def reference(w, x, r):
    w_hi, w_lo = split(w)
    w_hi_, w_lo_ = mxq(w_hi, 0, "e4m3"), mxq(w_lo, 0, "e4m3")
    x_hi, x_lo = split(x)
    x_hi_, x_lo_ = mxq(x_hi, 0, "e4m3"), mxq(x_lo, 0, "e4m3")
    y = x_hi_.T @ w_hi_ + x_lo_.T @ w_hi_ + x_hi_.T @ w_lo_
    out_0 = f64(r) + y
    return (out_0,) + planes(out_0)

@@ -1,0 +1,241 @@
+from contextlib import ExitStack
+
+import concourse.mybir as mybir
+
+K, N, T = 2048, 512, 512
+FLOPS = 3 * 2 * K * N * T
+
+F32 = mybir.dt.float32
+BF16 = mybir.dt.bfloat16
+I32 = mybir.dt.int32
+U32 = mybir.dt.uint32
+U8 = mybir.dt.uint8
+FP8X4 = mybir.dt.float8_e4m3fn_x4
+ALU = mybir.AluOpType
+
+P = 128
+PACK = 4
+K_PASS = P * PACK
+PASSES = K // K_PASS
+HI_MASK_PAIR = 0xFFF0FFF0 - (1 << 32)
+
+
+def tile_mix_split3_tm_pl_res_kernel(tc, w, x, r, out_0, out_1, out_2):
+    nc = tc.nc
+    with ExitStack() as ctx:
+        sb = ctx.enter_context(tc.tile_pool(name="sb", bufs=1))
+        ps = ctx.enter_context(tc.psum_pool(name="ps", bufs=1))
+        ctx.enter_context(tc.manual_schedule())
+
+        def load(name, src, g, c0, c1):
+            raw = sb.tile([P, PACK, c1 - c0], F32, name=name)
+            rows = src[g * K_PASS:(g + 1) * K_PASS, c0:c1]
+            nc.sync.dma_start(out=raw[:], in_=rows.rearrange("(p j) c -> p j c", j=PACK))
+            return raw
+
+        def upper(raw):
+            width = raw.shape[2]
+            return raw[:].bitcast(BF16)[:, :, 1:2 * width:2]
+
+        def make_chunk(name, words):
+            return {
+                "hi": sb.tile([P, PACK * words], BF16, name=name + "_hi", align_bytes=64),
+                "lo": sb.tile([P, PACK * words], BF16, name=name + "_lo", align_bytes=64),
+                "hi_c": sb.tile([P, words], U32, name=name + "_hic", align_bytes=64),
+                "hi_s": sb.tile([P, words], U8, name=name + "_his", align_bytes=64),
+                "lo_c": sb.tile([P, words], U32, name=name + "_loc", align_bytes=64),
+                "lo_s": sb.tile([P, words], U8, name=name + "_los", align_bytes=64),
+                "copies": [],
+                "subs": [],
+            }
+
+        def w_chunk(name, parts):
+            width = parts[0][2]
+            ch = make_chunk(name, width * len(parts))
+            for i, (raw, c0, width) in enumerate(parts):
+                span = slice(i * PACK * width, (i + 1) * PACK * width)
+                hi = ch["hi"][:, span].rearrange("p (c i j) -> p c j i", i=4, j=PACK)
+                lo = ch["lo"][:, span].rearrange("p (c i j) -> p c j i", i=4, j=PACK)
+                up = upper(raw)[:, :, c0:c0 + width].rearrange("p j (c i) -> p c j i", i=4)
+                full = raw[:, :, c0:c0 + width].rearrange("p j (c i) -> p c j i", i=4)
+                ch["copies"].append((hi, up))
+                ch["subs"].append((lo, full, hi))
+            return ch
+
+        def x_chunk(name, raw, h):
+            ch = make_chunk(name, 2 * P)
+            rs = slice(2 * h, 2 * h + 2)
+            up = upper(raw).rearrange("p j (m r) -> p m r j", r=4)[:, :, rs, :]
+            ch["copies"].append((ch["hi"][:].rearrange("p (r m j) -> p m r j", r=2, j=PACK), up))
+            full = raw[:].rearrange("p j (m r) -> p m j r", r=4)[:, :, :, rs]
+            ch["subs"].append((
+                ch["lo"][:].rearrange("p (r m j) -> p m j r", r=2, j=PACK),
+                full,
+                ch["hi"][:].rearrange("p (r m j) -> p m j r", r=2, j=PACK),
+            ))
+            return ch
+
+        wa0 = [load("wa0_%d" % i, w, 0, 128 * i, 128 * i + 128) for i in range(2)]
+        wa = [load("wa%d" % g, w, g, 0, 256) for g in range(1, PASSES)]
+        xs = [load("x%d" % g, x, g, 0, T) for g in range(PASSES)]
+        wb = [load("wb%d" % g, w, g, 256, 512) for g in range(2)]
+        res = sb.tile([P, PACK, N], F32, name="res")
+        nc.sync.dma_start(out=res[:], in_=r.rearrange("(p i) n -> p i n", i=PACK))
+        wb = wb + [load("wb%d" % g, w, g, 256, 512) for g in range(2, PASSES)]
+
+        a0 = make_chunk("a0", 256)
+        a0_halves = []
+        for i in range(2):
+            half = dict(a0)
+            half["hi"] = a0["hi"][:, 512 * i:512 * i + 512]
+            half["lo"] = a0["lo"][:, 512 * i:512 * i + 512]
+            half["hi_c"] = a0["hi_c"][:, 128 * i:128 * i + 128]
+            half["lo_c"] = a0["lo_c"][:, 128 * i:128 * i + 128]
+            half["hi_s"] = a0["hi_s"][:, 128 * i:128 * i + 128]
+            half["lo_s"] = a0["lo_s"][:, 128 * i:128 * i + 128]
+            hi = half["hi"].rearrange("p (c i j) -> p c j i", i=4, j=PACK)
+            lo = half["lo"].rearrange("p (c i j) -> p c j i", i=4, j=PACK)
+            half["copies"] = [(hi, upper(wa0[i]).rearrange("p j (c i) -> p c j i", i=4))]
+            half["subs"] = [(lo, wa0[i][:].rearrange("p j (c i) -> p c j i", i=4), hi)]
+            a0_halves.append(half)
+        a_ch = [a0] + [w_chunk("a%d" % g, [(wa[g - 1], 0, 256)]) for g in range(1, PASSES)]
+        x_ch = {(g, h): x_chunk("x%d_%d" % (g, h), xs[g], h) for g in range(PASSES) for h in range(2)}
+        b_groups = [(0, 1), (2, 3)]
+        c_groups = [(0, 1), (2,), (3,)]
+        b_ch = [w_chunk("b%d" % i, [(wb[g], 0, 128) for g in gs]) for i, gs in enumerate(b_groups)]
+        c_ch = [w_chunk("c%d" % i, [(wb[g], 128, 128) for g in gs]) for i, gs in enumerate(c_groups)]
+
+        banks = [ps.tile([P, 512], F32, name="bank%d" % b) for b in range(8)]
+        acc = {
+            "a": [banks[i][:, 0:256] for i in range(4)],
+            "b": [banks[4 + i][:, 0:128] for i in range(4)],
+            "c": [banks[i][:, 256:384] for i in range(4)],
+        }
+        cols = {"a": (0, 256), "b": (256, 384), "c": (384, 512)}
+        done = {}
+
+        def mm(part, i, xc, xk, wc, wk, w0):
+            width = cols[part][1] - cols[part][0]
+            count = done.get((part, i), 0)
+            done[(part, i)] = count + 1
+            m0 = P * (i % 2)
+            nc.tensor.matmul_mx(
+                out=acc[part][i],
+                lhsT=xc[xk + "_c"][:, m0:m0 + P].bitcast(FP8X4),
+                lhsT_scale=xc[xk + "_s"][:, m0:m0 + P],
+                rhs=wc[wk + "_c"][:, w0:w0 + width].bitcast(FP8X4),
+                rhs_scale=wc[wk + "_s"][:, w0:w0 + width],
+                start=(count == 0),
+                stop=(count == 3 * PASSES - 1),
+            )
+
+        def quant(ch, k):
+            nc.vector.quantize_mx(out=ch[k + "_c"][:].bitcast(FP8X4), scales=ch[k + "_s"][:], in_=ch[k][:])
+
+        def mask(ch):
+            words = ch["hi"][:].bitcast(I32)
+            nc.vector.tensor_scalar(out=words, in0=words, scalar1=HI_MASK_PAIR, scalar2=None, op0=ALU.bitwise_and)
+
+        out_rows = out_0.rearrange("(p i) n -> p i n", i=PACK)
+        out_words = out_1[0].rearrange("p n i -> p (n i)").bitcast(I32)
+        out_scales = out_2[0].bitcast(I32)
+        y_scales = sb.tile([P, N], U8, name="y_scales", align_bytes=64)
+        y, y_bf, y_codes = {}, {}, {}
+        for part, (n0, n1) in cols.items():
+            y[part] = sb.tile([P, PACK, n1 - n0], F32, name="y_" + part)
+            y_bf[part] = sb.tile([P, PACK * (n1 - n0)], BF16, name="ybf_" + part, align_bytes=64)
+            y_codes[part] = sb.tile([P, n1 - n0], U32, name="ycodes_" + part, align_bytes=64)
+
+        def add_res(part, i):
+            n0, n1 = cols[part]
+            nc.vector.tensor_tensor(out=y[part][:, i, :], in0=acc[part][i], in1=res[:, i, n0:n1], op=ALU.add)
+
+        def store_y(part):
+            n0, n1 = cols[part]
+            nc.sync.dma_start(out=out_rows[:, :, n0:n1], in_=y[part][:])
+
+        def cast_y(part, copy):
+            copy(
+                out=y_bf[part][:].rearrange("p (c i j) -> p c j i", i=4, j=PACK),
+                in_=y[part][:].rearrange("p j (c i) -> p c j i", i=4),
+            )
+
+        def quant_y(part):
+            n0, n1 = cols[part]
+            nc.vector.quantize_mx(out=y_codes[part][:].bitcast(FP8X4), scales=y_scales[:, n0:n1], in_=y_bf[part][:])
+            nc.sync.dma_start(out=out_words[:, n0:n1], in_=y_codes[part][:].bitcast(I32))
+
+        def x_after(g, h, k):
+            def run():
+                for i in (2 * h, 2 * h + 1):
+                    if k == "hi":
+                        mm("a", i, x_ch[g, h], "hi", a_ch[g], "hi", 0)
+                        mm("a", i, x_ch[g, h], "hi", a_ch[g], "lo", 0)
+                    else:
+                        mm("a", i, x_ch[g, h], "lo", a_ch[g], "hi", 0)
+            return run
+
+        def w_after(part, ch, gs, k):
+            def run():
+                for slot, g in enumerate(gs):
+                    for i in range(PACK):
+                        if k == "hi":
+                            mm(part, i, x_ch[g, i // 2], "hi", ch, "hi", 128 * slot)
+                            mm(part, i, x_ch[g, i // 2], "lo", ch, "hi", 128 * slot)
+                        else:
+                            mm(part, i, x_ch[g, i // 2], "hi", ch, "lo", 128 * slot)
+            return run
+
+        def nothing():
+            return None
+
+        steps = [(ch, nothing, nothing) for ch in a0_halves + a_ch[1:]]
+        steps += [(x_ch[g, h], x_after(g, h, "hi"), x_after(g, h, "lo")) for g in range(PASSES) for h in range(2)]
+        steps += [(ch, w_after("b", ch, gs, "hi"), w_after("b", ch, gs, "lo")) for ch, gs in zip(b_ch, b_groups)]
+        steps += [(ch, w_after("c", ch, gs, "hi"), w_after("c", ch, gs, "lo")) for ch, gs in zip(c_ch, c_groups)]
+        last = len(steps) - 1
+
+        def ep_a01():
+            add_res("a", 0)
+            add_res("a", 1)
+
+        def ep_a23():
+            add_res("a", 2)
+            add_res("a", 3)
+            store_y("a")
+            cast_y("a", nc.scalar.copy)
+
+        def ep_b():
+            quant_y("a")
+            for i in range(PACK):
+                add_res("b", i)
+            store_y("b")
+            cast_y("b", nc.scalar.copy)
+
+        extras = {last - 5: ep_a01, last - 4: ep_a23, last - 2: ep_b, last: lambda: quant_y("b")}
+
+        for s, (ch, after_hi, after_lo) in enumerate(steps):
+            copy = nc.vector.tensor_copy if s == 0 else nc.scalar.copy
+            for dst, src in ch["copies"]:
+                copy(out=dst, in_=src)
+
+        for s, (ch, after_hi, after_lo) in enumerate(steps):
+            mask(ch)
+            if s > 0:
+                quant(steps[s - 1][0], "lo")
+                steps[s - 1][2]()
+            quant(ch, "hi")
+            after_hi()
+            for lo, full, hi in ch["subs"]:
+                nc.vector.tensor_tensor(out=lo, in0=full, in1=hi, op=ALU.subtract)
+            extras.get(s, nothing)()
+        quant(steps[last][0], "lo")
+        steps[last][2]()
+        for i in range(PACK):
+            add_res("c", i)
+        store_y("c")
+        cast_y("c", nc.vector.tensor_copy)
+        quant_y("c")
+        for q in range(4):
+            queue = nc.scalar if q < 3 else nc.sync
+            queue.dma_start(out=out_scales[4 * q:4 * q + 4, :], in_=y_scales[32 * q:32 * q + 4, :].bitcast(I32))

@@ -18,6 +18,12 @@ PACK = 4
 K_PASS = P * PACK
 PASSES = K // K_PASS
 HI_MASK_PAIR = 0xFFF0FFF0 - (1 << 32)
+RUN = 2
+
+COLS = {"a": (0, 256), "b": (256, 384), "c": (384, 512)}
+W_FRONT = [
+    (0, (0, 128)), (0, (128, 256)), (1, (0, 128)), (1, (128, 256, 384)), (2, (0, 128, 384)), (3, (0, 128, 384)),
+]
 
 
 def tile_mix_split3_tm_pl_res_kernel(tc, w, x, r, out_0, out_1, out_2):
@@ -34,76 +40,66 @@ def tile_mix_split3_tm_pl_res_kernel(tc, w, x, r, out_0, out_1, out_2):
             return raw
 
         def upper(raw):
-            width = raw.shape[2]
-            return raw[:].bitcast(BF16)[:, :, 1:2 * width:2]
+            return raw[:].bitcast(BF16)[:, :, 1:2 * raw.shape[2]:2]
 
-        def make_chunk(name, words):
+        def planes(name):
+            made = {}
+            for k in ("hi", "lo"):
+                for g in range(PASSES):
+                    made[k, g] = (
+                        sb.tile([P, 512], U32, name="%s_%s_codes%d" % (name, k, g), align_bytes=64),
+                        sb.tile([P, 512], U8, name="%s_%s_scales%d" % (name, k, g), align_bytes=64),
+                    )
+            return made
+
+        w_mx, x_mx = planes("w"), planes("x")
+
+        def chunk(name, mx, g, c0, c1, packed, up, full):
+            hi = sb.tile([P, PACK * (c1 - c0)], BF16, name=name + "_hi", align_bytes=64)
+            lo = sb.tile([P, PACK * (c1 - c0)], BF16, name=name + "_lo", align_bytes=64)
             return {
-                "hi": sb.tile([P, PACK * words], BF16, name=name + "_hi", align_bytes=64),
-                "lo": sb.tile([P, PACK * words], BF16, name=name + "_lo", align_bytes=64),
-                "hi_c": sb.tile([P, words], U32, name=name + "_hic", align_bytes=64),
-                "hi_s": sb.tile([P, words], U8, name=name + "_his", align_bytes=64),
-                "lo_c": sb.tile([P, words], U32, name=name + "_loc", align_bytes=64),
-                "lo_s": sb.tile([P, words], U8, name=name + "_los", align_bytes=64),
-                "copies": [],
-                "subs": [],
+                "hi": hi, "lo": lo, "hi_v": packed(hi), "lo_v": packed(lo), "up": up, "full": full,
+                "mx": {k: (mx[k, g][0][:, c0:c1], mx[k, g][1][:, c0:c1]) for k in ("hi", "lo")},
             }
 
-        def w_chunk(name, parts):
-            width = parts[0][2]
-            ch = make_chunk(name, width * len(parts))
-            for i, (raw, c0, width) in enumerate(parts):
-                span = slice(i * PACK * width, (i + 1) * PACK * width)
-                hi = ch["hi"][:, span].rearrange("p (c i j) -> p c j i", i=4, j=PACK)
-                lo = ch["lo"][:, span].rearrange("p (c i j) -> p c j i", i=4, j=PACK)
-                up = upper(raw)[:, :, c0:c0 + width].rearrange("p j (c i) -> p c j i", i=4)
-                full = raw[:, :, c0:c0 + width].rearrange("p j (c i) -> p c j i", i=4)
-                ch["copies"].append((hi, up))
-                ch["subs"].append((lo, full, hi))
-            return ch
+        def side_by_side(t):
+            return t.rearrange("p (c i j) -> p c j i", i=RUN, j=PACK)
 
-        def x_chunk(name, raw, h):
-            ch = make_chunk(name, 2 * P)
-            rs = slice(2 * h, 2 * h + 2)
-            up = upper(raw).rearrange("p j (m r) -> p m r j", r=4)[:, :, rs, :]
-            ch["copies"].append((ch["hi"][:].rearrange("p (r m j) -> p m r j", r=2, j=PACK), up))
-            full = raw[:].rearrange("p j (m r) -> p m j r", r=4)[:, :, :, rs]
-            ch["subs"].append((
-                ch["lo"][:].rearrange("p (r m j) -> p m j r", r=2, j=PACK),
-                full,
-                ch["hi"][:].rearrange("p (r m j) -> p m j r", r=2, j=PACK),
-            ))
-            return ch
+        def by_rows(t):
+            return t.rearrange("p j (c i) -> p c j i", i=RUN)
 
-        wa0 = [load("wa0_%d" % i, w, 0, 128 * i, 128 * i + 128) for i in range(2)]
-        wa = [load("wa%d" % g, w, g, 0, 256) for g in range(1, PASSES)]
-        xs = [load("x%d" % g, x, g, 0, T) for g in range(PASSES)]
-        wb = [load("wb%d" % g, w, g, 256, 512) for g in range(2)]
+        def w_chunks(g, cuts):
+            c0, c1 = cuts[0], cuts[-1]
+            raw = load("w%d_%d" % (g, c0), w, g, c0, c1)
+            made = []
+            for a, b in zip(cuts[:-1], cuts[1:]):
+                made.append(chunk(
+                    "w%d_%d" % (g, a), w_mx, g, a, b, lambda t: side_by_side(t[:]),
+                    by_rows(upper(raw)[:, :, a - c0:b - c0]), by_rows(raw[:, :, a - c0:b - c0]),
+                ))
+            return made
+
+        def x_chunks(g):
+            raw = load("x%d" % g, x, g, 0, T)
+            made = []
+            for h in range(2):
+                rs = slice(2 * h, 2 * h + 2)
+                made.append(chunk(
+                    "x%d_%d" % (g, h), x_mx, g, 256 * h, 256 * h + 256,
+                    lambda t: t[:].rearrange("p (i m j) -> p m j i", i=2, j=PACK),
+                    upper(raw).rearrange("p j (m i) -> p m j i", i=4)[:, :, :, rs],
+                    raw[:].rearrange("p j (m i) -> p m j i", i=4)[:, :, :, rs],
+                ))
+            return made
+
+        front = []
+        for g, cuts in W_FRONT:
+            front += w_chunks(g, cuts)
+        xs = [x_chunks(g) for g in range(PASSES)]
         res = sb.tile([P, PACK, N], F32, name="res")
         nc.sync.dma_start(out=res[:], in_=r.rearrange("(p i) n -> p i n", i=PACK))
-        wb = wb + [load("wb%d" % g, w, g, 256, 512) for g in range(2, PASSES)]
-
-        a0 = make_chunk("a0", 256)
-        a0_halves = []
-        for i in range(2):
-            half = dict(a0)
-            half["hi"] = a0["hi"][:, 512 * i:512 * i + 512]
-            half["lo"] = a0["lo"][:, 512 * i:512 * i + 512]
-            half["hi_c"] = a0["hi_c"][:, 128 * i:128 * i + 128]
-            half["lo_c"] = a0["lo_c"][:, 128 * i:128 * i + 128]
-            half["hi_s"] = a0["hi_s"][:, 128 * i:128 * i + 128]
-            half["lo_s"] = a0["lo_s"][:, 128 * i:128 * i + 128]
-            hi = half["hi"].rearrange("p (c i j) -> p c j i", i=4, j=PACK)
-            lo = half["lo"].rearrange("p (c i j) -> p c j i", i=4, j=PACK)
-            half["copies"] = [(hi, upper(wa0[i]).rearrange("p j (c i) -> p c j i", i=4))]
-            half["subs"] = [(lo, wa0[i][:].rearrange("p j (c i) -> p c j i", i=4), hi)]
-            a0_halves.append(half)
-        a_ch = [a0] + [w_chunk("a%d" % g, [(wa[g - 1], 0, 256)]) for g in range(1, PASSES)]
-        x_ch = {(g, h): x_chunk("x%d_%d" % (g, h), xs[g], h) for g in range(PASSES) for h in range(2)}
-        b_groups = [(0, 1), (2, 3)]
-        c_groups = [(0, 1), (2,), (3,)]
-        b_ch = [w_chunk("b%d" % i, [(wb[g], 0, 128) for g in gs]) for i, gs in enumerate(b_groups)]
-        c_ch = [w_chunk("c%d" % i, [(wb[g], 128, 128) for g in gs]) for i, gs in enumerate(c_groups)]
+        b0, c0 = w_chunks(0, (256, 384, 512))
+        cs = [c0] + [w_chunks(g, (384, 512))[0] for g in range(1, PASSES)]
 
         banks = [ps.tile([P, 512], F32, name="bank%d" % b) for b in range(8)]
         acc = {
@@ -111,131 +107,137 @@ def tile_mix_split3_tm_pl_res_kernel(tc, w, x, r, out_0, out_1, out_2):
             "b": [banks[4 + i][:, 0:128] for i in range(4)],
             "c": [banks[i][:, 256:384] for i in range(4)],
         }
-        cols = {"a": (0, 256), "b": (256, 384), "c": (384, 512)}
         done = {}
 
-        def mm(part, i, xc, xk, wc, wk, w0):
-            width = cols[part][1] - cols[part][0]
+        def mm(part, i, g, xk, wk):
+            n0, n1 = COLS[part]
             count = done.get((part, i), 0)
-            done[(part, i)] = count + 1
-            m0 = P * (i % 2)
+            done[part, i] = count + 1
             nc.tensor.matmul_mx(
                 out=acc[part][i],
-                lhsT=xc[xk + "_c"][:, m0:m0 + P].bitcast(FP8X4),
-                lhsT_scale=xc[xk + "_s"][:, m0:m0 + P],
-                rhs=wc[wk + "_c"][:, w0:w0 + width].bitcast(FP8X4),
-                rhs_scale=wc[wk + "_s"][:, w0:w0 + width],
+                lhsT=x_mx[xk, g][0][:, P * i:P * i + P].bitcast(FP8X4),
+                lhsT_scale=x_mx[xk, g][1][:, P * i:P * i + P],
+                rhs=w_mx[wk, g][0][:, n0:n1].bitcast(FP8X4),
+                rhs_scale=w_mx[wk, g][1][:, n0:n1],
                 start=(count == 0),
                 stop=(count == 3 * PASSES - 1),
             )
 
         def quant(ch, k):
-            nc.vector.quantize_mx(out=ch[k + "_c"][:].bitcast(FP8X4), scales=ch[k + "_s"][:], in_=ch[k][:])
-
-        def mask(ch):
-            words = ch["hi"][:].bitcast(I32)
-            nc.vector.tensor_scalar(out=words, in0=words, scalar1=HI_MASK_PAIR, scalar2=None, op0=ALU.bitwise_and)
+            codes, scales = ch["mx"][k]
+            nc.vector.quantize_mx(out=codes.bitcast(FP8X4), scales=scales, in_=ch[k][:])
 
         out_rows = out_0.rearrange("(p i) n -> p i n", i=PACK)
         out_words = out_1[0].rearrange("p n i -> p (n i)").bitcast(I32)
         out_scales = out_2[0].bitcast(I32)
         y_scales = sb.tile([P, N], U8, name="y_scales", align_bytes=64)
-        y, y_bf, y_codes = {}, {}, {}
-        for part, (n0, n1) in cols.items():
+        y_codes = sb.tile([P, N], U32, name="y_codes", align_bytes=64)
+        y, y_bf = {}, {}
+        for part, (n0, n1) in COLS.items():
             y[part] = sb.tile([P, PACK, n1 - n0], F32, name="y_" + part)
             y_bf[part] = sb.tile([P, PACK * (n1 - n0)], BF16, name="ybf_" + part, align_bytes=64)
-            y_codes[part] = sb.tile([P, n1 - n0], U32, name="ycodes_" + part, align_bytes=64)
 
-        def add_res(part, i):
-            n0, n1 = cols[part]
-            nc.vector.tensor_tensor(out=y[part][:, i, :], in0=acc[part][i], in1=res[:, i, n0:n1], op=ALU.add)
+        def add_res(part, tiles):
+            n0, n1 = COLS[part]
+            for i in tiles:
+                nc.vector.tensor_tensor(out=y[part][:, i, :], in0=acc[part][i], in1=res[:, i, n0:n1], op=ALU.add)
 
         def store_y(part):
-            n0, n1 = cols[part]
+            n0, n1 = COLS[part]
             nc.sync.dma_start(out=out_rows[:, :, n0:n1], in_=y[part][:])
 
-        def cast_y(part, copy):
-            copy(
-                out=y_bf[part][:].rearrange("p (c i j) -> p c j i", i=4, j=PACK),
-                in_=y[part][:].rearrange("p j (c i) -> p c j i", i=4),
+        def cast_y(part, copy, a, b):
+            copy(out=side_by_side(y_bf[part][:, PACK * a:PACK * b]), in_=by_rows(y[part][:, :, a:b]))
+
+        def quant_y(part, a, b):
+            n0 = COLS[part][0]
+            nc.vector.quantize_mx(
+                out=y_codes[:, n0 + a:n0 + b].bitcast(FP8X4),
+                scales=y_scales[:, n0 + a:n0 + b],
+                in_=y_bf[part][:, PACK * a:PACK * b],
             )
 
-        def quant_y(part):
-            n0, n1 = cols[part]
-            nc.vector.quantize_mx(out=y_codes[part][:].bitcast(FP8X4), scales=y_scales[:, n0:n1], in_=y_bf[part][:])
-            nc.sync.dma_start(out=out_words[:, n0:n1], in_=y_codes[part][:].bitcast(I32))
+        def store_words(n0, n1):
+            nc.sync.dma_start(out=out_words[:, n0:n1], in_=y_codes[:, n0:n1].bitcast(I32))
 
-        def x_after(g, h, k):
-            def run():
+        def x_ready(g, h, k):
+            for part in ("a", "b") if g >= 1 else ("a",):
                 for i in (2 * h, 2 * h + 1):
-                    if k == "hi":
-                        mm("a", i, x_ch[g, h], "hi", a_ch[g], "hi", 0)
-                        mm("a", i, x_ch[g, h], "hi", a_ch[g], "lo", 0)
-                    else:
-                        mm("a", i, x_ch[g, h], "lo", a_ch[g], "hi", 0)
-            return run
+                    for wk in ("hi", "lo") if k == "hi" else ("hi",):
+                        mm(part, i, g, k, wk)
 
-        def w_after(part, ch, gs, k):
-            def run():
-                for slot, g in enumerate(gs):
-                    for i in range(PACK):
-                        if k == "hi":
-                            mm(part, i, x_ch[g, i // 2], "hi", ch, "hi", 128 * slot)
-                            mm(part, i, x_ch[g, i // 2], "lo", ch, "hi", 128 * slot)
-                        else:
-                            mm(part, i, x_ch[g, i // 2], "hi", ch, "lo", 128 * slot)
-            return run
+        def w_ready(part, g, k, tiles=range(PACK)):
+            for i in tiles:
+                for xk in ("hi", "lo") if k == "hi" else ("hi",):
+                    mm(part, i, g, xk, k)
 
-        def nothing():
-            return None
+        def mask(ch):
+            words = ch["hi"][:].bitcast(I32)
+            nc.vector.tensor_scalar(out=words, in0=words, scalar1=HI_MASK_PAIR, scalar2=None, op0=ALU.bitwise_and)
 
-        steps = [(ch, nothing, nothing) for ch in a0_halves + a_ch[1:]]
-        steps += [(x_ch[g, h], x_after(g, h, "hi"), x_after(g, h, "lo")) for g in range(PASSES) for h in range(2)]
-        steps += [(ch, w_after("b", ch, gs, "hi"), w_after("b", ch, gs, "lo")) for ch, gs in zip(b_ch, b_groups)]
-        steps += [(ch, w_after("c", ch, gs, "hi"), w_after("c", ch, gs, "lo")) for ch, gs in zip(c_ch, c_groups)]
-        last = len(steps) - 1
+        def subtract(ch):
+            nc.vector.tensor_tensor(out=ch["lo_v"], in0=ch["full"], in1=ch["hi_v"], op=ALU.subtract)
 
-        def ep_a01():
-            add_res("a", 0)
-            add_res("a", 1)
-
-        def ep_a23():
-            add_res("a", 2)
-            add_res("a", 3)
-            store_y("a")
-            cast_y("a", nc.scalar.copy)
-
-        def ep_b():
-            quant_y("a")
-            for i in range(PACK):
-                add_res("b", i)
-            store_y("b")
-            cast_y("b", nc.scalar.copy)
-
-        extras = {last - 5: ep_a01, last - 4: ep_a23, last - 2: ep_b, last: lambda: quant_y("b")}
-
-        for s, (ch, after_hi, after_lo) in enumerate(steps):
+        steps = [(ch, None) for ch in front]
+        steps += [(xs[g][h], (g, h)) for g in range(PASSES) for h in range(2)]
+        for s, ch in enumerate([step[0] for step in steps] + cs + [b0]):
             copy = nc.vector.tensor_copy if s == 0 else nc.scalar.copy
-            for dst, src in ch["copies"]:
-                copy(out=dst, in_=src)
+            copy(out=ch["hi_v"], in_=ch["up"])
 
-        for s, (ch, after_hi, after_lo) in enumerate(steps):
-            mask(ch)
+        def finish(step):
+            for k in ("hi", "lo"):
+                quant(step[0], k)
+                if step[1] is not None:
+                    x_ready(step[1][0], step[1][1], k)
+
+        for s, step in enumerate(steps):
+            mask(step[0])
             if s > 0:
-                quant(steps[s - 1][0], "lo")
-                steps[s - 1][2]()
-            quant(ch, "hi")
-            after_hi()
-            for lo, full, hi in ch["subs"]:
-                nc.vector.tensor_tensor(out=lo, in0=full, in1=hi, op=ALU.subtract)
-            extras.get(s, nothing)()
-        quant(steps[last][0], "lo")
-        steps[last][2]()
-        for i in range(PACK):
-            add_res("c", i)
+                finish(steps[s - 1])
+            subtract(step[0])
+        add_res("a", (0, 1))
+
+        mask(cs[0])
+        mask(cs[1])
+        finish(steps[-1])
+        for g in (0, 1):
+            quant(cs[g], "hi")
+            w_ready("c", g, "hi", (0, 1))
+        subtract(cs[0])
+        add_res("a", (2, 3))
+        store_y("a")
+        cast_y("a", nc.scalar.copy, 0, 256)
+        for g in (0, 1):
+            w_ready("c", g, "hi", (2, 3))
+        subtract(cs[1])
+        mask(cs[2])
+        mask(cs[3])
+        for g, k in ((0, "lo"), (1, "lo"), (2, "hi"), (3, "hi")):
+            quant(cs[g], k)
+            w_ready("c", g, k)
+        subtract(cs[2])
+        subtract(cs[3])
+        mask(b0)
+        for g in (2, 3):
+            quant(cs[g], "lo")
+            w_ready("c", g, "lo")
+        quant(b0, "hi")
+        w_ready("b", 0, "hi")
+        subtract(b0)
+        quant_y("a", 0, 256)
+        store_words(0, 256)
+        quant(b0, "lo")
+        w_ready("b", 0, "lo")
+        add_res("c", range(PACK))
         store_y("c")
-        cast_y("c", nc.vector.tensor_copy)
-        quant_y("c")
+        cast_y("c", nc.scalar.copy, 0, 128)
+        add_res("b", range(PACK))
+        store_y("b")
+        for a in (0, 64):
+            cast_y("b", nc.vector.tensor_copy, a, a + 64)
+        quant_y("c", 0, 128)
+        quant_y("b", 0, 128)
+        store_words(256, 512)
         for q in range(4):
             queue = nc.scalar if q < 3 else nc.sync
             queue.dma_start(out=out_scales[4 * q:4 * q + 4, :], in_=y_scales[32 * q:32 * q + 4, :].bitcast(I32))

@@ -1,6 +1,7 @@
 from contextlib import ExitStack
 
 import concourse.mybir as mybir
+from concourse.masks import make_identity
 
 K, N, T = 2048, 512, 512
 FLOPS = 3 * 2 * K * N * T
@@ -17,6 +18,9 @@ P = 128
 PACK = 4
 K_PASS = P * PACK
 PASSES = K // K_PASS
+HI_MASK = 0xFFF00000 - (1 << 32)
+SIGN_BIT = -(1 << 31)
+ACT = mybir.ActivationFunctionType
 HI_MASK_PAIR = 0xFFF0FFF0 - (1 << 32)
 RUN = 2
 
@@ -94,8 +98,16 @@ def tile_mix_split3_tm_pl_res_kernel(tc, w, x, r, out_0, out_1, out_2):
 
         front = []
         for g, cuts in W_FRONT:
+            if g == 3:
+                x3 = load("x3", x, 3, 0, T)
             front += w_chunks(g, cuts)
-        xs = [x_chunks(g) for g in range(PASSES)]
+        xs = [x_chunks(g) for g in range(PASSES - 1)]
+        ident = sb.tile([P, P], F32, name="ident")
+        make_identity(nc, ident[:])
+        neg_hi = sb.tile([P, PACK, T], F32, name="neg_hi")
+        hi3 = sb.tile([P, PACK * T], BF16, name="hi3", align_bytes=64)
+        lo3 = sb.tile([P, PACK * T], BF16, name="lo3", align_bytes=64)
+        lo3_t = [sb.tile([P, K_PASS], BF16, name="lo3_t%d" % a) for a in range(4)]
         res = sb.tile([P, PACK, N], F32, name="res")
         nc.sync.dma_start(out=res[:], in_=r.rearrange("(p i) n -> p i n", i=PACK))
         b0, c0 = w_chunks(0, (256, 384, 512))
@@ -160,11 +172,10 @@ def tile_mix_split3_tm_pl_res_kernel(tc, w, x, r, out_0, out_1, out_2):
         def store_words(n0, n1):
             nc.sync.dma_start(out=out_words[:, n0:n1], in_=y_codes[:, n0:n1].bitcast(I32))
 
-        def x_ready(g, h, k):
-            for part in ("a", "b") if g >= 1 else ("a",):
-                for i in (2 * h, 2 * h + 1):
-                    for wk in ("hi", "lo") if k == "hi" else ("hi",):
-                        mm(part, i, g, k, wk)
+        def x_ready(part, g, tiles, k):
+            for i in tiles:
+                for wk in ("hi", "lo") if k == "hi" else ("hi",):
+                    mm(part, i, g, k, wk)
 
         def w_ready(part, g, k, tiles=range(PACK)):
             for i in tiles:
@@ -178,28 +189,124 @@ def tile_mix_split3_tm_pl_res_kernel(tc, w, x, r, out_0, out_1, out_2):
         def subtract(ch):
             nc.vector.tensor_tensor(out=ch["lo_v"], in0=ch["full"], in1=ch["hi_v"], op=ALU.subtract)
 
-        steps = [(ch, None) for ch in front]
-        steps += [(xs[g][h], (g, h)) for g in range(PASSES) for h in range(2)]
-        for s, ch in enumerate([step[0] for step in steps] + cs + [b0]):
-            copy = nc.vector.tensor_copy if s == 0 else nc.scalar.copy
+        def take_upper(ch, copy=nc.scalar.copy):
             copy(out=ch["hi_v"], in_=ch["up"])
 
-        def finish(step):
-            for k in ("hi", "lo"):
-                quant(step[0], k)
-                if step[1] is not None:
-                    x_ready(step[1][0], step[1][1], k)
+        def negated_hi():
+            nc.vector.tensor_scalar(
+                out=neg_hi[:].bitcast(I32), in0=x3[:].bitcast(I32), scalar1=HI_MASK, scalar2=SIGN_BIT,
+                op0=ALU.bitwise_and, op1=ALU.bitwise_xor,
+            )
 
-        for s, step in enumerate(steps):
-            mask(step[0])
-            if s > 0:
-                finish(steps[s - 1])
-            subtract(step[0])
+        def subtract_turned(a):
+            for j in range(PACK):
+                for src, first in ((x3, True), (neg_hi, False)):
+                    nc.tensor.matmul(
+                        out=banks[4 + a][:, P * j:P * j + P], lhsT=src[:, j, P * a:P * a + P], rhs=ident[:],
+                        start=first, stop=not first, is_transpose=True,
+                    )
+
+        def round_turned(a):
+            nc.scalar.copy(
+                out=lo3_t[a][:].rearrange("q (u p e) -> q u p e", u=2, e=2),
+                in_=banks[4 + a][:].rearrange("q (u e p) -> q u p e", u=2, e=2),
+            )
+
+        def turn_back(b):
+            for u in range(2):
+                for e in range(2):
+                    at = 256 * u + P * e
+                    nc.tensor.transpose(
+                        banks[4 + 2 * b][:, at:at + P], lo3_t[2 * b + e][:].bitcast(F32)[:, P * u:P * u + P], ident[:]
+                    )
+
+        def fetch_back(b):
+            nc.scalar.copy(
+                out=lo3[:].bitcast(F32).rearrange("p (i m u) -> p i m u", i=4, u=2)[:, :, 64 * b:64 * b + 64, :],
+                in_=banks[4 + 2 * b][:].rearrange("p (u m i) -> p i m u", u=2, i=4),
+            )
+
+        def cast_hi3(h, e):
+            ms = slice(64 * e, 64 * e + 64)
+            nc.scalar.activation(
+                out=hi3[:, 1024 * h:1024 * h + 1024].rearrange("p (i m j) -> p m j i", i=2, j=PACK)[:, ms],
+                in_=neg_hi[:].rearrange("p j (m i) -> p m j i", i=4)[:, ms, :, 2 * h:2 * h + 2],
+                func=ACT.Copy, scale=-1.0,
+            )
+
+        def quant3(k, src, a, b):
+            nc.vector.quantize_mx(
+                out=x_mx[k, 3][0][:, P * a:P * b].bitcast(FP8X4), scales=x_mx[k, 3][1][:, P * a:P * b],
+                in_=src[:, K_PASS * a:K_PASS * b],
+            )
+
+        def advance(ch, before, g=None, h=None, parts=()):
+            mask(ch)
+            for k in ("hi", "lo"):
+                quant(before, k)
+                for part in parts:
+                    x_ready(part, g, (2 * h, 2 * h + 1), k)
+            subtract(ch)
+
+        take_upper(front[0], nc.vector.tensor_copy)
+        for ch in front[1:-2]:
+            take_upper(ch)
+        mask(front[0])
+        subtract(front[0])
+        for s in range(1, len(front) - 3):
+            advance(front[s], front[s - 1])
+        negated_hi()
+        cast_hi3(0, 0)
+        take_upper(front[-2])
+        take_upper(front[-1])
+        cast_hi3(0, 1)
+        for s in range(len(front) - 3, len(front)):
+            advance(front[s], front[s - 1])
+        for a in range(4):
+            subtract_turned(a)
+        take_upper(xs[0][0])
+        take_upper(xs[0][1])
+        round_turned(0)
+        round_turned(1)
+        take_upper(xs[1][0])
+        round_turned(2)
+        round_turned(3)
+        take_upper(xs[1][1])
+        advance(xs[0][0], front[-1])
+        advance(xs[0][1], xs[0][0], 0, 0, "a")
+        turn_back(0)
+        turn_back(1)
+        advance(xs[1][0], xs[0][1], 0, 1, "a")
+        fetch_back(0)
+        cast_hi3(1, 0)
+        fetch_back(1)
+        take_upper(xs[2][0])
+        cast_hi3(1, 1)
+        for ch in xs[2][1:] + cs + [b0]:
+            take_upper(ch)
+        advance(xs[1][1], xs[1][0], 1, 0, "ab")
+        quant3("lo", lo3, 0, 4)
+        for part in "ab":
+            x_ready(part, 3, range(PACK), "lo")
+        quant3("hi", hi3, 0, 2)
+        for part in "ab":
+            x_ready(part, 3, (0, 1), "hi")
+        advance(xs[2][0], xs[1][1], 1, 1, "ab")
+        quant3("hi", hi3, 2, 4)
+        x_ready("a", 3, (2, 3), "hi")
+        advance(xs[2][1], xs[2][0], 2, 0, "a")
+        x_ready("b", 3, (2, 3), "hi")
+        for k in ("hi", "lo"):
+            x_ready("b", 2, (0, 1), k)
         add_res("a", (0, 1))
 
         mask(cs[0])
         mask(cs[1])
-        finish(steps[-1])
+        for k in ("hi", "lo"):
+            quant(xs[2][1], k)
+            x_ready("a", 2, (2, 3), k)
+        for k in ("hi", "lo"):
+            x_ready("b", 2, (2, 3), k)
         for g in (0, 1):
             quant(cs[g], "hi")
             w_ready("c", g, "hi", (0, 1))

from contextlib import ExitStack

import concourse.mybir as mybir
from concourse.masks import make_identity

K, N, T = 2048, 512, 512
FLOPS = 3 * 2 * K * N * T

F32 = mybir.dt.float32
BF16 = mybir.dt.bfloat16
I32 = mybir.dt.int32
U32 = mybir.dt.uint32
U8 = mybir.dt.uint8
FP8X4 = mybir.dt.float8_e4m3fn_x4
ALU = mybir.AluOpType

P = 128
PACK = 4
K_PASS = P * PACK
PASSES = K // K_PASS
HI_MASK = 0xFFF00000 - (1 << 32)
SIGN_BIT = -(1 << 31)
ACT = mybir.ActivationFunctionType
HI_MASK_PAIR = 0xFFF0FFF0 - (1 << 32)
RUN = 2

COLS = {"a": (0, 256), "b": (256, 384), "c": (384, 512)}
W_FRONT = [
    (0, (0, 128)), (0, (128, 256)), (1, (0, 128)), (1, (128, 256, 384)), (2, (0, 128, 384)), (3, (0, 128, 384)),
]


def tile_mix_split3_tm_pl_res_kernel(tc, w, x, r, out_0, out_1, out_2):
    nc = tc.nc
    with ExitStack() as ctx:
        sb = ctx.enter_context(tc.tile_pool(name="sb", bufs=1))
        ps = ctx.enter_context(tc.psum_pool(name="ps", bufs=1))
        ctx.enter_context(tc.manual_schedule())

        def load(name, src, g, c0, c1):
            raw = sb.tile([P, PACK, c1 - c0], F32, name=name)
            rows = src[g * K_PASS:(g + 1) * K_PASS, c0:c1]
            nc.sync.dma_start(out=raw[:], in_=rows.rearrange("(p j) c -> p j c", j=PACK))
            return raw

        def upper(raw):
            return raw[:].bitcast(BF16)[:, :, 1:2 * raw.shape[2]:2]

        def planes(name):
            made = {}
            for k in ("hi", "lo"):
                for g in range(PASSES):
                    made[k, g] = (
                        sb.tile([P, 512], U32, name="%s_%s_codes%d" % (name, k, g), align_bytes=64),
                        sb.tile([P, 512], U8, name="%s_%s_scales%d" % (name, k, g), align_bytes=64),
                    )
            return made

        w_mx, x_mx = planes("w"), planes("x")

        def chunk(name, mx, g, c0, c1, packed, up, full):
            hi = sb.tile([P, PACK * (c1 - c0)], BF16, name=name + "_hi", align_bytes=64)
            lo = sb.tile([P, PACK * (c1 - c0)], BF16, name=name + "_lo", align_bytes=64)
            return {
                "hi": hi, "lo": lo, "hi_v": packed(hi), "lo_v": packed(lo), "up": up, "full": full,
                "mx": {k: (mx[k, g][0][:, c0:c1], mx[k, g][1][:, c0:c1]) for k in ("hi", "lo")},
            }

        def side_by_side(t):
            return t.rearrange("p (c i j) -> p c j i", i=RUN, j=PACK)

        def by_rows(t):
            return t.rearrange("p j (c i) -> p c j i", i=RUN)

        def w_chunks(g, cuts):
            c0, c1 = cuts[0], cuts[-1]
            raw = load("w%d_%d" % (g, c0), w, g, c0, c1)
            made = []
            for a, b in zip(cuts[:-1], cuts[1:]):
                made.append(chunk(
                    "w%d_%d" % (g, a), w_mx, g, a, b, lambda t: side_by_side(t[:]),
                    by_rows(upper(raw)[:, :, a - c0:b - c0]), by_rows(raw[:, :, a - c0:b - c0]),
                ))
            return made

        def x_chunks(g):
            raw = load("x%d" % g, x, g, 0, T)
            made = []
            for h in range(2):
                rs = slice(2 * h, 2 * h + 2)
                made.append(chunk(
                    "x%d_%d" % (g, h), x_mx, g, 256 * h, 256 * h + 256,
                    lambda t: t[:].rearrange("p (i m j) -> p m j i", i=2, j=PACK),
                    upper(raw).rearrange("p j (m i) -> p m j i", i=4)[:, :, :, rs],
                    raw[:].rearrange("p j (m i) -> p m j i", i=4)[:, :, :, rs],
                ))
            return made

        front = []
        for g, cuts in W_FRONT:
            if g == 3:
                x3 = load("x3", x, 3, 0, T)
            front += w_chunks(g, cuts)
        xs = [x_chunks(g) for g in range(PASSES - 1)]
        ident = sb.tile([P, P], F32, name="ident")
        make_identity(nc, ident[:])
        neg_hi = sb.tile([P, PACK, T], F32, name="neg_hi")
        hi3 = sb.tile([P, PACK * T], BF16, name="hi3", align_bytes=64)
        lo3 = sb.tile([P, PACK * T], BF16, name="lo3", align_bytes=64)
        lo3_t = [sb.tile([P, K_PASS], BF16, name="lo3_t%d" % a) for a in range(4)]
        res = sb.tile([P, PACK, N], F32, name="res")
        nc.sync.dma_start(out=res[:], in_=r.rearrange("(p i) n -> p i n", i=PACK))
        b0, c0 = w_chunks(0, (256, 384, 512))
        cs = [c0] + [w_chunks(g, (384, 512))[0] for g in range(1, PASSES)]

        banks = [ps.tile([P, 512], F32, name="bank%d" % b) for b in range(8)]
        acc = {
            "a": [banks[i][:, 0:256] for i in range(4)],
            "b": [banks[4 + i][:, 0:128] for i in range(4)],
            "c": [banks[i][:, 256:384] for i in range(4)],
        }
        done = {}

        def mm(part, i, g, xk, wk):
            n0, n1 = COLS[part]
            count = done.get((part, i), 0)
            done[part, i] = count + 1
            nc.tensor.matmul_mx(
                out=acc[part][i],
                lhsT=x_mx[xk, g][0][:, P * i:P * i + P].bitcast(FP8X4),
                lhsT_scale=x_mx[xk, g][1][:, P * i:P * i + P],
                rhs=w_mx[wk, g][0][:, n0:n1].bitcast(FP8X4),
                rhs_scale=w_mx[wk, g][1][:, n0:n1],
                start=(count == 0),
                stop=(count == 3 * PASSES - 1),
            )

        def quant(ch, k):
            codes, scales = ch["mx"][k]
            nc.vector.quantize_mx(out=codes.bitcast(FP8X4), scales=scales, in_=ch[k][:])

        out_rows = out_0.rearrange("(p i) n -> p i n", i=PACK)
        out_words = out_1[0].rearrange("p n i -> p (n i)").bitcast(I32)
        out_scales = out_2[0].bitcast(I32)
        y_scales = sb.tile([P, N], U8, name="y_scales", align_bytes=64)
        y_codes = sb.tile([P, N], U32, name="y_codes", align_bytes=64)
        y, y_bf = {}, {}
        for part, (n0, n1) in COLS.items():
            y[part] = sb.tile([P, PACK, n1 - n0], F32, name="y_" + part)
            y_bf[part] = sb.tile([P, PACK * (n1 - n0)], BF16, name="ybf_" + part, align_bytes=64)

        def add_res(part, tiles):
            n0, n1 = COLS[part]
            for i in tiles:
                nc.vector.tensor_tensor(out=y[part][:, i, :], in0=acc[part][i], in1=res[:, i, n0:n1], op=ALU.add)

        def store_y(part):
            n0, n1 = COLS[part]
            nc.sync.dma_start(out=out_rows[:, :, n0:n1], in_=y[part][:])

        def cast_y(part, copy, a, b):
            copy(out=side_by_side(y_bf[part][:, PACK * a:PACK * b]), in_=by_rows(y[part][:, :, a:b]))

        def quant_y(part, a, b):
            n0 = COLS[part][0]
            nc.vector.quantize_mx(
                out=y_codes[:, n0 + a:n0 + b].bitcast(FP8X4),
                scales=y_scales[:, n0 + a:n0 + b],
                in_=y_bf[part][:, PACK * a:PACK * b],
            )

        def store_words(n0, n1):
            nc.sync.dma_start(out=out_words[:, n0:n1], in_=y_codes[:, n0:n1].bitcast(I32))

        def x_ready(part, g, tiles, k):
            for i in tiles:
                for wk in ("hi", "lo") if k == "hi" else ("hi",):
                    mm(part, i, g, k, wk)

        def w_ready(part, g, k, tiles=range(PACK)):
            for i in tiles:
                for xk in ("hi", "lo") if k == "hi" else ("hi",):
                    mm(part, i, g, xk, k)

        def mask(ch):
            words = ch["hi"][:].bitcast(I32)
            nc.vector.tensor_scalar(out=words, in0=words, scalar1=HI_MASK_PAIR, scalar2=None, op0=ALU.bitwise_and)

        def subtract(ch):
            nc.vector.tensor_tensor(out=ch["lo_v"], in0=ch["full"], in1=ch["hi_v"], op=ALU.subtract)

        def take_upper(ch, copy=nc.scalar.copy):
            copy(out=ch["hi_v"], in_=ch["up"])

        def negated_hi():
            nc.vector.tensor_scalar(
                out=neg_hi[:].bitcast(I32), in0=x3[:].bitcast(I32), scalar1=HI_MASK, scalar2=SIGN_BIT,
                op0=ALU.bitwise_and, op1=ALU.bitwise_xor,
            )

        def subtract_turned(a):
            for j in range(PACK):
                for src, first in ((x3, True), (neg_hi, False)):
                    nc.tensor.matmul(
                        out=banks[4 + a][:, P * j:P * j + P], lhsT=src[:, j, P * a:P * a + P], rhs=ident[:],
                        start=first, stop=not first, is_transpose=True,
                    )

        def round_turned(a):
            nc.scalar.copy(
                out=lo3_t[a][:].rearrange("q (u p e) -> q u p e", u=2, e=2),
                in_=banks[4 + a][:].rearrange("q (u e p) -> q u p e", u=2, e=2),
            )

        def turn_back(b):
            for u in range(2):
                for e in range(2):
                    at = 256 * u + P * e
                    nc.tensor.transpose(
                        banks[4 + 2 * b][:, at:at + P], lo3_t[2 * b + e][:].bitcast(F32)[:, P * u:P * u + P], ident[:]
                    )

        def fetch_back(b):
            nc.scalar.copy(
                out=lo3[:].bitcast(F32).rearrange("p (i m u) -> p i m u", i=4, u=2)[:, :, 64 * b:64 * b + 64, :],
                in_=banks[4 + 2 * b][:].rearrange("p (u m i) -> p i m u", u=2, i=4),
            )

        def cast_hi3(h, e):
            ms = slice(64 * e, 64 * e + 64)
            nc.scalar.activation(
                out=hi3[:, 1024 * h:1024 * h + 1024].rearrange("p (i m j) -> p m j i", i=2, j=PACK)[:, ms],
                in_=neg_hi[:].rearrange("p j (m i) -> p m j i", i=4)[:, ms, :, 2 * h:2 * h + 2],
                func=ACT.Copy, scale=-1.0,
            )

        def quant3(k, src, a, b):
            nc.vector.quantize_mx(
                out=x_mx[k, 3][0][:, P * a:P * b].bitcast(FP8X4), scales=x_mx[k, 3][1][:, P * a:P * b],
                in_=src[:, K_PASS * a:K_PASS * b],
            )

        def advance(ch, before, g=None, h=None, parts=()):
            mask(ch)
            for k in ("hi", "lo"):
                quant(before, k)
                for part in parts:
                    x_ready(part, g, (2 * h, 2 * h + 1), k)
            subtract(ch)

        take_upper(front[0], nc.vector.tensor_copy)
        for ch in front[1:-2]:
            take_upper(ch)
        mask(front[0])
        subtract(front[0])
        for s in range(1, len(front) - 3):
            advance(front[s], front[s - 1])
        negated_hi()
        cast_hi3(0, 0)
        take_upper(front[-2])
        take_upper(front[-1])
        cast_hi3(0, 1)
        for s in range(len(front) - 3, len(front)):
            advance(front[s], front[s - 1])
        for a in range(4):
            subtract_turned(a)
        take_upper(xs[0][0])
        take_upper(xs[0][1])
        round_turned(0)
        round_turned(1)
        take_upper(xs[1][0])
        round_turned(2)
        round_turned(3)
        take_upper(xs[1][1])
        advance(xs[0][0], front[-1])
        advance(xs[0][1], xs[0][0], 0, 0, "a")
        turn_back(0)
        turn_back(1)
        advance(xs[1][0], xs[0][1], 0, 1, "a")
        fetch_back(0)
        cast_hi3(1, 0)
        fetch_back(1)
        take_upper(xs[2][0])
        cast_hi3(1, 1)
        for ch in xs[2][1:] + cs + [b0]:
            take_upper(ch)
        advance(xs[1][1], xs[1][0], 1, 0, "ab")
        quant3("lo", lo3, 0, 4)
        for part in "ab":
            x_ready(part, 3, range(PACK), "lo")
        quant3("hi", hi3, 0, 2)
        for part in "ab":
            x_ready(part, 3, (0, 1), "hi")
        advance(xs[2][0], xs[1][1], 1, 1, "ab")
        quant3("hi", hi3, 2, 4)
        x_ready("a", 3, (2, 3), "hi")
        advance(xs[2][1], xs[2][0], 2, 0, "a")
        x_ready("b", 3, (2, 3), "hi")
        for k in ("hi", "lo"):
            x_ready("b", 2, (0, 1), k)
        add_res("a", (0, 1))

        mask(cs[0])
        mask(cs[1])
        for k in ("hi", "lo"):
            quant(xs[2][1], k)
            x_ready("a", 2, (2, 3), k)
        for k in ("hi", "lo"):
            x_ready("b", 2, (2, 3), k)
        for g in (0, 1):
            quant(cs[g], "hi")
            w_ready("c", g, "hi", (0, 1))
        subtract(cs[0])
        add_res("a", (2, 3))
        store_y("a")
        cast_y("a", nc.scalar.copy, 0, 256)
        for g in (0, 1):
            w_ready("c", g, "hi", (2, 3))
        subtract(cs[1])
        mask(cs[2])
        mask(cs[3])
        for g, k in ((0, "lo"), (1, "lo"), (2, "hi"), (3, "hi")):
            quant(cs[g], k)
            w_ready("c", g, k)
        subtract(cs[2])
        subtract(cs[3])
        mask(b0)
        for g in (2, 3):
            quant(cs[g], "lo")
            w_ready("c", g, "lo")
        quant(b0, "hi")
        w_ready("b", 0, "hi")
        subtract(b0)
        quant_y("a", 0, 256)
        store_words(0, 256)
        quant(b0, "lo")
        w_ready("b", 0, "lo")
        add_res("c", range(PACK))
        store_y("c")
        cast_y("c", nc.scalar.copy, 0, 128)
        add_res("b", range(PACK))
        store_y("b")
        for a in (0, 64):
            cast_y("b", nc.vector.tensor_copy, a, a + 64)
        quant_y("c", 0, 128)
        quant_y("b", 0, 128)
        store_words(256, 512)
        for q in range(4):
            queue = nc.scalar if q < 3 else nc.sync
            queue.dma_start(out=out_scales[4 * q:4 * q + 4, :], in_=y_scales[32 * q:32 * q + 4, :].bitcast(I32))
